import numpy as np
import ml_dtypes

BF16 = ml_dtypes.bfloat16


def bf(x):
    return np.asarray(x, np.float32).astype(BF16)


def f32(x):
    return np.asarray(x, np.float32)


def f64(x):
    return np.asarray(x).astype(np.float64)


def striped(idx):
    return np.tile(idx.reshape(-1, 16).T, (8, 1))


def rows(idx, k):
    return np.tile(idx, (k, 1))


def look(tab, idx):
    return np.take_along_axis(f64(tab), rows(idx, len(tab)), axis=1)


K, S, V, N = 512, 2048, 1024, 1024


def setup_inputs():
    return {"tab": f32(np.random.standard_normal((2, K, S))), "offs": striped(np.random.permutation(S)[:N])}


def reference(tab, offs):
    idx = offs[:16].T.reshape(-1)
    x = ((look(tab[0], idx) - 0.125) * 1.5) * (np.maximum(look(tab[1], idx), 0.0))
    return x

@@ -1,0 +1,37 @@
+import concourse.mybir as mybir
+
+F32, U16 = mybir.dt.float32, mybir.dt.uint16
+RELU = mybir.ActivationFunctionType.Relu
+SUBTRACT, MULT = mybir.AluOpType.subtract, mybir.AluOpType.mult
+SHIFT, SCALE = 0.125, 1.5
+P = 128
+
+
+def tile_lookup_vg_nrmrelu_out_kernel(tc, tab, offs, out):
+    nc = tc.nc
+    rows, places = tab.shape[1], tab.shape[2]
+    entries = out.shape[1]
+    with (
+        tc.tile_pool(name="lists", bufs=1) as lists,
+        tc.tile_pool(name="windows", bufs=rows // P) as windows,
+        tc.tile_pool(name="picked", bufs=2) as picked,
+    ):
+        offsets = lists.tile([P, entries // 16], U16, name="offsets")
+        nc.sync.dma_start(offsets[:], offs)
+
+        for block in range(rows // P):
+            block_rows = slice(block * P, (block + 1) * P)
+            values = windows.tile([P, places], F32, name="values")
+            gates = windows.tile([P, places], F32, name="gates")
+            nc.sync.dma_start(values[:], tab[0, block_rows, :])
+            nc.sync.dma_start(gates[:], tab[1, block_rows, :])
+
+            scaled = picked.tile([P, entries], F32, name="scaled")
+            opened = picked.tile([P, entries], F32, name="opened")
+            product = picked.tile([P, entries], F32, name="product")
+            nc.vector.tensor_scalar(
+                scaled[:], values[:].indirect(offsets[:]), SHIFT, SCALE, op0=SUBTRACT, op1=MULT
+            )
+            nc.scalar.activation(opened[:], gates[:].indirect(offsets[:]), RELU)
+            nc.vector.tensor_tensor(product[:], scaled[:], opened[:], MULT)
+            nc.sync.dma_start(out[block_rows, :], product[:])

@@ -14,24 +14,26 @@ def tile_lookup_vg_nrmrelu_out_kernel(tc, tab, offs, out):
     with (
         tc.tile_pool(name="lists", bufs=1) as lists,
         tc.tile_pool(name="windows", bufs=rows // P) as windows,
-        tc.tile_pool(name="picked", bufs=2) as picked,
+        tc.tile_pool(name="picked", bufs=rows // P) as picked,
     ):
         offsets = lists.tile([P, entries // 16], U16, name="offsets")
         nc.sync.dma_start(offsets[:], offs)
 
+        values, gates = [], []
         for block in range(rows // P):
             block_rows = slice(block * P, (block + 1) * P)
-            values = windows.tile([P, places], F32, name="values")
-            gates = windows.tile([P, places], F32, name="gates")
-            nc.sync.dma_start(values[:], tab[0, block_rows, :])
-            nc.sync.dma_start(gates[:], tab[1, block_rows, :])
+            values.append(windows.tile([P, places], F32, name="values"))
+            gates.append(windows.tile([P, places], F32, name="gates"))
+            nc.sync.dma_start(values[block][:], tab[0, block_rows, :])
+            nc.sync.dma_start(gates[block][:], tab[1, block_rows, :])
 
+        for block in range(rows // P):
             scaled = picked.tile([P, entries], F32, name="scaled")
             opened = picked.tile([P, entries], F32, name="opened")
             product = picked.tile([P, entries], F32, name="product")
             nc.vector.tensor_scalar(
-                scaled[:], values[:].indirect(offsets[:]), SHIFT, SCALE, op0=SUBTRACT, op1=MULT
+                scaled[:], values[block][:].indirect(offsets[:]), SHIFT, SCALE, op0=SUBTRACT, op1=MULT
             )
-            nc.scalar.activation(opened[:], gates[:].indirect(offsets[:]), RELU)
+            nc.scalar.activation(opened[:], gates[block][:].indirect(offsets[:]), RELU)
             nc.vector.tensor_tensor(product[:], scaled[:], opened[:], MULT)
-            nc.sync.dma_start(out[block_rows, :], product[:])
+            nc.sync.dma_start(out[block * P : (block + 1) * P, :], product[:])

@@ -5,6 +5,7 @@ RELU = mybir.ActivationFunctionType.Relu
 SUBTRACT, MULT = mybir.AluOpType.subtract, mybir.AluOpType.mult
 SHIFT, SCALE = 0.125, 1.5
 P = 128
+LAST_PIECES = 4
 
 
 def tile_lookup_vg_nrmrelu_out_kernel(tc, tab, offs, out):
@@ -34,6 +35,11 @@ def tile_lookup_vg_nrmrelu_out_kernel(tc, tab, offs, out):
             nc.vector.tensor_scalar(
                 scaled[:], values[block][:].indirect(offsets[:]), SHIFT, SCALE, op0=SUBTRACT, op1=MULT
             )
-            nc.scalar.activation(opened[:], gates[block][:].indirect(offsets[:]), RELU)
-            nc.vector.tensor_tensor(product[:], scaled[:], opened[:], MULT)
-            nc.sync.dma_start(out[block * P : (block + 1) * P, :], product[:])
+            pieces = LAST_PIECES if block == rows // P - 1 else 1
+            piece = entries // pieces
+            for start in range(0, entries, piece):
+                columns = slice(start, start + piece)
+                piece_offsets = offsets[:, start // 16 : (start + piece) // 16]
+                nc.scalar.activation(opened[:, columns], gates[block][:].indirect(piece_offsets), RELU)
+                nc.vector.tensor_tensor(product[:, columns], scaled[:, columns], opened[:, columns], MULT)
+                nc.sync.dma_start(out[block * P : (block + 1) * P, columns], product[:, columns])

@@ -18,14 +18,14 @@ def tile_lookup_vg_nrmrelu_out_kernel(tc, tab, offs, out):
         tc.tile_pool(name="picked", bufs=rows // P) as picked,
     ):
         offsets = lists.tile([P, entries // 16], U16, name="offsets")
-        nc.sync.dma_start(offsets[:], offs)
-
         values, gates = [], []
         for block in range(rows // P):
             block_rows = slice(block * P, (block + 1) * P)
             values.append(windows.tile([P, places], F32, name="values"))
             gates.append(windows.tile([P, places], F32, name="gates"))
             nc.sync.dma_start(values[block][:], tab[0, block_rows, :])
+            if block == 0:
+                nc.sync.dma_start(offsets[:], offs)
             nc.sync.dma_start(gates[block][:], tab[1, block_rows, :])
 
         for block in range(rows // P):

import concourse.mybir as mybir

F32, U16 = mybir.dt.float32, mybir.dt.uint16
RELU = mybir.ActivationFunctionType.Relu
SUBTRACT, MULT = mybir.AluOpType.subtract, mybir.AluOpType.mult
SHIFT, SCALE = 0.125, 1.5
P = 128
LAST_PIECES = 4


def tile_lookup_vg_nrmrelu_out_kernel(tc, tab, offs, out):
    nc = tc.nc
    rows, places = tab.shape[1], tab.shape[2]
    entries = out.shape[1]
    with (
        tc.tile_pool(name="lists", bufs=1) as lists,
        tc.tile_pool(name="windows", bufs=rows // P) as windows,
        tc.tile_pool(name="picked", bufs=rows // P) as picked,
    ):
        offsets = lists.tile([P, entries // 16], U16, name="offsets")
        values, gates = [], []
        for block in range(rows // P):
            block_rows = slice(block * P, (block + 1) * P)
            values.append(windows.tile([P, places], F32, name="values"))
            gates.append(windows.tile([P, places], F32, name="gates"))
            nc.sync.dma_start(values[block][:], tab[0, block_rows, :])
            if block == 0:
                nc.sync.dma_start(offsets[:], offs)
            nc.sync.dma_start(gates[block][:], tab[1, block_rows, :])

        for block in range(rows // P):
            scaled = picked.tile([P, entries], F32, name="scaled")
            opened = picked.tile([P, entries], F32, name="opened")
            product = picked.tile([P, entries], F32, name="product")
            nc.vector.tensor_scalar(
                scaled[:], values[block][:].indirect(offsets[:]), SHIFT, SCALE, op0=SUBTRACT, op1=MULT
            )
            pieces = LAST_PIECES if block == rows // P - 1 else 1
            piece = entries // pieces
            for start in range(0, entries, piece):
                columns = slice(start, start + piece)
                piece_offsets = offsets[:, start // 16 : (start + piece) // 16]
                nc.scalar.activation(opened[:, columns], gates[block][:].indirect(piece_offsets), RELU)
                nc.vector.tensor_tensor(product[:, columns], scaled[:, columns], opened[:, columns], MULT)
                nc.sync.dma_start(out[block * P : (block + 1) * P, columns], product[:, columns])
